import numpy as np
import ml_dtypes


def mxq(x, axis, fmt="e4m3"):
    dtype, down = {"e4m3": (ml_dtypes.float8_e4m3fn, 7), "e5m2": (ml_dtypes.float8_e5m2, 14)}[fmt]
    v = np.moveaxis(np.asarray(x, np.float32).astype(ml_dtypes.bfloat16).astype(np.float64), axis, -1)
    blocks = v.reshape(v.shape[:-1] + (-1, 32))
    amax = np.abs(blocks).max(-1, keepdims=True)
    byte = np.maximum(np.where(amax > 0, np.frexp(amax)[1] - 1 + 127, 0) - down, 1)
    scale = np.exp2(byte - 127.0)
    codes = (blocks / scale).astype(np.float32).astype(dtype).astype(np.float64)
    return np.moveaxis((codes * scale).reshape(v.shape), -1, axis)


WIDE = False


def mx_kscale(k):
    if not WIDE:
        return np.ones(k)
    levels = np.array([10, -10, 5, -5, 0])
    if k % 512:
        return np.exp2(np.random.permutation(np.resize(levels, k // 32))).repeat(32)
    a = np.empty((k // 512, 16))
    for p in range(k // 512):
        a[p, :8] = np.random.permutation(np.resize(levels, 8))
        for g in range(8):
            far = levels[np.abs(levels - a[p, g]) >= 10]
            a[p, g + 8] = far[np.random.randint(len(far))]
    return np.exp2(a.ravel()).repeat(32)


def f64(x):
    return np.asarray(x).astype(np.float64)


def striped(idx):
    return np.tile(idx.reshape(-1, 16).T, (8, 1)).astype(np.uint16)


def unstriped(offs):
    return offs[:16].T.reshape(-1).astype(np.int64)


E2M1 = np.array([0.0, 0.5, 1.0, 1.5, 2.0, 3.0, 4.0, 6.0, -0.0, -0.5, -1.0, -1.5, -2.0, -3.0, -4.0, -6.0])


def pack_weight(w, fmt):
    k, n = w.shape
    w = f64(np.asarray(w, np.float32).astype(ml_dtypes.bfloat16)).reshape(k // 32, 32, n)
    amax = np.abs(w).max(1)
    if fmt == "e4m3":
        byte = np.frexp(amax)[1] - 1 + 127 - 7
    else:
        mant, ex = np.frexp(amax / 6.0)
        byte = np.where(mant > 0.5, ex, ex - 1) + 127
    byte = np.clip(np.where(amax > 0, byte, 1), 1, 254)
    scaled = (w * np.exp2(127.0 - byte)[:, None, :]).reshape(k, n).astype(np.float32)
    by_word = np.ascontiguousarray(scaled.reshape(k // 512, 128, 4, n).transpose(0, 1, 3, 2))
    if fmt == "e4m3":
        words = by_word.astype(ml_dtypes.float8_e4m3fn).view(np.uint8)
    else:
        c = by_word.astype(ml_dtypes.float4_e2m1fn).view(np.uint8) & 0xF
        words = (c[..., 0::2] | (c[..., 1::2] << 4)).reshape(k // 512, 128, 2 * n)
    return np.ascontiguousarray(words), np.ascontiguousarray(byte.astype(np.uint8).reshape(k // 512, 16, n))


def unpack_weight(words, scales, fmt):
    g, _, n = scales.shape
    words = np.ascontiguousarray(words).reshape(g, 128, n, -1)
    if fmt == "e4m3":
        vals = words.view(ml_dtypes.float8_e4m3fn).astype(np.float64)
    else:
        nib = np.empty((g, 128, n, 4), np.uint8)
        nib[..., 0::2] = words & 0xF
        nib[..., 1::2] = words >> 4
        vals = E2M1[nib]
    vals = vals * np.repeat(np.exp2(scales.astype(np.float64) - 127.0), 8, axis=1)[..., None]
    return vals.transpose(0, 1, 3, 2).reshape(g * 512, n)


def gelu(v):
    return 0.5 * v * (1.0 + np.tanh(np.sqrt(2.0 / np.pi) * (v + 0.044715 * v**3)))


def bf(x):
    return np.asarray(x, np.float32).astype(ml_dtypes.bfloat16)


def planes(Y):
    n, m = Y.shape
    b = f64(bf(Y)).reshape(n // 32, 32, m)
    amax = np.abs(b).max(1)
    byte = np.clip(np.where(amax > 0, np.frexp(amax)[1] - 1 + 127 - 7, 1), 1, 254)
    codes = (b * np.exp2(127.0 - byte)[:, None, :]).reshape(n, m).astype(np.float32).astype(ml_dtypes.float8_e4m3fn).view(np.uint8)
    words = codes.reshape(n // 512, 128, 4, m).transpose(0, 1, 3, 2)
    return np.ascontiguousarray(words), np.ascontiguousarray(byte.astype(np.uint8).reshape(n // 512, 16, m))


K, H, N, T, S, T2, P = 1024, 512, 384, 4096, 1024, 2048, 1024

def setup_inputs():
    n = np.random.standard_normal
    s = mx_kscale(K)[:, None]
    u = mx_kscale(H)[:, None]
    d = {}
    d["tab_words"], d["tab_scales"] = pack_weight(n((K, T)) * s, "e4m3")
    d["offs"] = striped(np.random.permutation(T)[:S])
    d["offs2"] = striped(np.random.permutation(T2)[:S])
    d["offs3"] = striped(np.random.permutation(T2)[:P])
    d["w1"] = (0.8 * n((K, H)) / K ** 0.5 / s).astype(np.float32)
    d["w2_words"], d["w2_scales"] = pack_weight(0.8 * n((K, H)) / K ** 0.5 / s, "e2m1")
    d["gain"] = (np.exp(0.3 * n(H)) * u[:, 0]).astype(np.float32)
    d["wgs"] = np.exp(0.3 * n((128, S))).astype(np.float32)
    d["page0"] = (n((H, T2)) * u).astype(np.float32)
    d["rd"] = np.exp(0.3 * n(H)).astype(np.float32)
    d["w4_words"], d["w4_scales"] = pack_weight(n((H, N)) / H ** 0.5 / u, "e4m3")
    d["cush"] = n((N, P)).astype(np.float32)
    d["scl"] = np.exp(0.4 * n(N)).astype(np.float32)
    return d

def reference(tab_words, tab_scales, offs, offs2, offs3, w1, w2_words, w2_scales, gain, wgs, page0, rd, w4_words, w4_scales, cush, scl):
    v = unpack_weight(tab_words, tab_scales, "e4m3")[:, unstriped(offs)]
    track = mxq(f64(w1), 0, "e4m3").T @ v
    spin = unpack_weight(w2_words, w2_scales, "e2m1").T @ v
    h = f64(gain)[:, None] * (spin * np.square(track) - track)
    page = f64(page0).copy()
    page[:, unstriped(offs2)] = np.tile(f64(wgs), (H // 128, 1)) * h
    x = page[:, unstriped(offs3)] * f64(rd)[:, None]
    e = unpack_weight(w4_words, w4_scales, "e4m3").T @ mxq(x, 0, "e4m3")
    y = f64(scl)[:, None] * np.maximum(e, f64(cush))
    words, scales = planes(page)
    return y, page, words, scales

from contextlib import ExitStack

import concourse.mybir as mybir
from concourse.masks import make_identity

K, H, N, T, S, T2, PK = 1024, 512, 384, 4096, 1024, 2048, 1024
FLOPS = 2 * K * H * S * 2 + 2 * H * N * PK

F32 = mybir.dt.float32
BF16 = mybir.dt.bfloat16
I32 = mybir.dt.int32
U32 = mybir.dt.uint32
U16 = mybir.dt.uint16
U8 = mybir.dt.uint8
FP8X4 = mybir.dt.float8_e4m3fn_x4
FP4X4 = mybir.dt.float4_e2m1fn_x4
MULT = mybir.AluOpType.mult
MAX = mybir.AluOpType.max
COPY = mybir.ActivationFunctionType.Copy
SQUARE = mybir.ActivationFunctionType.Square

P = 128
PACK = 4
QUADS = 4
PASSES = K // (P * PACK)
BANK = 512
BLOCKS = S // P
PER_COL = 16


def tile_list_snooker_position_page_kernel(
    tc, tab_words, tab_scales, offs, offs2, offs3, w1, w2_words, w2_scales, gain, wgs, page0, rd,
    w4_words, w4_scales, cush, scl, out_0, out_1, out_2, out_3,
):
    nc = tc.nc
    with ExitStack() as ctx:
        keep = ctx.enter_context(tc.tile_pool(name="keep", bufs=1))
        psum = ctx.enter_context(tc.psum_pool(name="psum", bufs=1))

        pick = keep.tile([P, S // PER_COL], U16, name="pick")
        put = keep.tile([P, S // PER_COL], U16, name="put")
        read = keep.tile([P, PK // PER_COL], U16, name="read")
        ident = keep.tile([P, P], F32, name="ident")
        v_words = [[keep.tile([P, BANK], U32, name="v_words%d%d" % (a, h), align_bytes=64) for h in range(2)] for a in range(PASSES)]
        v_rows = keep.tile([P, S], U8, name="v_rows", align_bytes=64)
        v_plane = [keep.tile([P, S], U8, name="v_plane%d" % a, align_bytes=64) for a in range(PASSES)]
        w1_codes = [keep.tile([P, H], U32, name="w1_codes%d" % a, align_bytes=64) for a in range(PASSES)]
        w1_plane = [keep.tile([P, H], U8, name="w1_plane%d" % a, align_bytes=64) for a in range(PASSES)]
        w2_codes = keep.tile([P, PASSES, 2 * H], U8, name="w2_codes", align_bytes=64)
        w2_plane = keep.tile([P, PASSES, H], U8, name="w2_plane", align_bytes=64)
        w4_codes = keep.tile([P, N], I32, name="w4_codes", align_bytes=64)
        w4_plane = keep.tile([P, N], U8, name="w4_plane", align_bytes=64)
        gain_sb = keep.tile([P, PACK], F32, name="gain_sb")
        rd_sb = keep.tile([P, PACK], F32, name="rd_sb")
        scl_sb = keep.tile([P, N // P], F32, name="scl_sb")
        page = [keep.tile([P, T2], F32, name="page%d" % t) for t in range(PACK)]
        wgs_first = keep.tile([P, S], F32, name="wgs_first")
        wgs_rest = keep.tile([P, PACK - 1, S], F32, name="wgs_rest")
        cush_sb = keep.tile([P, N // P, PK], F32, name="cush_sb")
        cubic = [keep.tile([P, PACK, P], F32, name="cubic%d" % b) for b in range(BLOCKS)]
        minus_track = [keep.tile([P, PACK, P], F32, name="minus_track%d" % b) for b in range(BLOCKS)]
        h_sb = [keep.tile([P, S], F32, name="h%d" % t) for t in range(PACK)]

        page_rows_in = page0.rearrange("(p t) m -> t p m", t=PACK)
        page_rows_out = out_1.rearrange("(p t) m -> t p m", t=PACK)
        wgs_rows = wgs.rearrange("(q t) j -> q t j", t=PACK)

        with tc.tile_pool(name="head", bufs=1) as head:
            tab_rows = head.tile([P, T // 4], I32, name="tab_rows")
            tab = [head.tile([P, T], I32, name="tab%d" % a) for a in range(PASSES)]
            w1_raw = [head.tile([P, PACK, H], F32, name="w1_raw%d" % a) for a in range(PASSES)]
            w1_bf = [head.tile([P, H, PACK], BF16, name="w1_bf%d" % a, align_bytes=64) for a in range(PASSES)]

            nc.vector.memset(tab_rows[32:64, :], 0)
            nc.vector.memset(tab_rows[64:128, :], 0)
            nc.vector.memset(w2_plane[:].bitcast(I32), 0)
            for a in range(PASSES):
                nc.vector.memset(v_plane[a][:].bitcast(I32), 0)
            nc.vector.memset(w4_plane[:].bitcast(I32), 0)

            nc.sync.dma_start(pick[:], offs)
            nc.sync.dma_start(tab_rows[0:32, :], tab_scales.rearrange("a q t -> (a q) t").bitcast(I32))
            for a in range(PASSES):
                nc.sync.dma_start(w1_raw[a][:], w1[a * 512 : (a + 1) * 512, :].rearrange("(p j) c -> p j c", j=PACK))
            nc.sync.dma_start(tab[0][:], tab_words[0].rearrange("p t i -> p (t i)").bitcast(I32))
            nc.sync.dma_start(w2_codes[:].bitcast(I32), w2_words.rearrange("a p c -> p a c").bitcast(I32))
            nc.sync.dma_start(tab[1][:], tab_words[1].rearrange("p t i -> p (t i)").bitcast(I32))
            nc.sync.dma_start(gain_sb[:], gain.rearrange("(p t) -> p t", t=PACK))
            nc.sync.dma_start(put[:], offs2)
            nc.sync.dma_start(page[0][:], page_rows_in[0])
            for q in (0, 2, 1, 3):
                nc.sync.dma_start(wgs_first[32 * q : 32 * q + 32, :], wgs_rows[:, 0, :])
            nc.sync.dma_start(read[:], offs3)
            nc.sync.dma_start(rd_sb[:], rd.rearrange("(p t) -> p t", t=PACK))
            nc.sync.dma_start(page[1][:], page_rows_in[1])
            for q in (0, 2, 1, 3):
                nc.sync.dma_start(wgs_rest[32 * q : 32 * q + 32, :, :], wgs_rows[:, 1:, :])
            nc.sync.dma_start(page[2][:], page_rows_in[2])
            nc.sync.dma_start(page[3][:], page_rows_in[3])
            nc.sync.dma_start(w4_codes[:], w4_words[0].rearrange("p c i -> p (c i)").bitcast(I32))
            nc.sync.dma_start(cush_sb[:], cush.rearrange("(b p) j -> p b j", p=P))
            for q in range(QUADS):
                nc.sync.dma_start(w4_plane[32 * q : 32 * q + 4, :].bitcast(I32), w4_scales[0, 4 * q : 4 * q + 4, :].bitcast(I32))
            with nc.allow_non_contiguous_dma(reason="one scale a partition"):
                nc.sync.dma_start(scl_sb[:], scl.rearrange("(b p) -> p b", p=P))

            for q in range(QUADS):
                nc.gpsimd.dma_start(
                    w2_plane[32 * q : 32 * q + 4, :, :].bitcast(I32),
                    w2_scales[:, 4 * q : 4 * q + 4, :].rearrange("a r c -> r a c").bitcast(I32),
                )
            make_identity(nc, ident[:])

            nc.vector.tensor_copy(v_rows[:], tab_rows[:].bitcast(U8).indirect(pick[:]))
            for a in range(PASSES):
                for q in range(QUADS):
                    row = 16 * a + 4 * q
                    nc.gpsimd.dma_start(v_plane[a][32 * q : 32 * q + 4, :].bitcast(I32), v_rows[row : row + 4, :].bitcast(I32))

            for a in range(PASSES):
                nc.scalar.copy(w1_bf[a][:], w1_raw[a][:].rearrange("p j c -> p c j"))
                nc.vector.quantize_mx(
                    out=w1_codes[a][:].bitcast(FP8X4), scales=w1_plane[a][:], in_=w1_bf[a][:].rearrange("p c j -> p (c j)")
                )
            for a in range(PASSES):
                for h in range(2):
                    cols = slice(h * 32, (h + 1) * 32)
                    nc.vector.tensor_copy(v_words[a][h][:], tab[a][:].bitcast(U32).indirect(pick[:, cols]))


        late = ctx.enter_context(tc.tile_pool(name="late", bufs=1))

        def first_stage(b):
            h, cols = b // 4, slice((b % 4) * P, (b % 4 + 1) * P)
            track = psum.tile([P, BANK], F32, name="track", tag="acc", bufs=6)
            spin = psum.tile([P, BANK], F32, name="spin", tag="acc", bufs=6)
            for a in range(PASSES):
                lhs = v_words[a][h][:, cols].bitcast(FP8X4)
                lhs_scale = v_plane[a][:, b * P : (b + 1) * P]
                nc.tensor.matmul_mx(track[:], lhsT=lhs, lhsT_scale=lhs_scale, rhs=w1_codes[a][:].bitcast(FP8X4),
                                    rhs_scale=w1_plane[a][:], start=(a == 0), stop=(a == PASSES - 1))
                nc.tensor.matmul_mx(spin[:], lhsT=lhs, lhsT_scale=lhs_scale, rhs=w2_codes[:, a, :].bitcast(FP4X4),
                                    rhs_scale=w2_plane[:, a, :], start=(a == 0), stop=(a == PASSES - 1))
            track_dealt = track[:].rearrange("j (m t) -> j t m", t=PACK)
            square = late.tile([P, PACK, P], F32, name="square", bufs=2)
            nc.scalar.activation(square[:], track_dealt, SQUARE)
            nc.scalar.activation(minus_track[b][:], track_dealt, COPY, scale=-1.0)
            nc.vector.tensor_tensor(cubic[b][:], spin[:].rearrange("j (m t) -> j t m", t=PACK), square[:], MULT)

        def turn(t, b0, b1):
            bank = psum.tile([P, BANK], F32, name="turned", tag="turned", bufs=2)
            for b in range(b0, b1):
                dst = bank[:, (b - b0) * P : (b - b0 + 1) * P]
                nc.tensor.matmul(dst, lhsT=minus_track[b][:, t, :], rhs=ident[:], is_transpose=True, start=True, stop=False)
                nc.tensor.matmul(dst, lhsT=cubic[b][:, t, :], rhs=ident[:], is_transpose=True, start=False, stop=True)
            nc.scalar.activation(h_sb[t][:, b0 * P : b1 * P], bank[:, : (b1 - b0) * P], COPY, scale=gain_sb[:, t : t + 1])

        def scatter(t, j0, j1):
            weights = wgs_first[:, j0:j1] if t == 0 else wgs_rest[:, t - 1, j0:j1]
            nc.vector.tensor_tensor(page[t][:].indirect(put[:, j0 // PER_COL : j1 // PER_COL]), h_sb[t][:, j0:j1], weights, MULT)

        page_pairs = [late.tile([P, 2, BANK, 2], BF16, name="page_pairs%d" % c) for c in range(4)]
        x_pairs = [late.tile([P, 2, BANK, 2], BF16, name="x_pairs%d" % h) for h in range(2)]
        picked = [[late.tile([P, BANK], F32, name="picked%d%d" % (t, h)) for h in range(2)] for t in range(PACK)]
        page_scales = late.tile([P, T2], U8, name="page_scales", align_bytes=64)
        x_codes = [late.tile([P, BANK], U32, name="x_codes%d" % h, align_bytes=64) for h in range(2)]
        x_plane = [late.tile([P, BANK], U8, name="x_plane%d" % h, align_bytes=64) for h in range(2)]
        page_woven = [late.tile([P, BANK, 2], F32, name="page_woven%d" % c, align_bytes=64) for c in range(4)]
        x_woven = [late.tile([P, BANK, 2], F32, name="x_woven%d" % h, align_bytes=64) for h in range(2)]

        def gather(t, h):
            nc.vector.tensor_copy(picked[t][h][:], page[t][:].indirect(read[:, h * 32 : (h + 1) * 32]))

        def round_page(t, c):
            nc.scalar.copy(page_pairs[c][:, t // 2, :, t % 2], page[t][:, c * BANK : (c + 1) * BANK])

        def round_x(t, h):
            nc.scalar.activation(x_pairs[h][:, t // 2, :, t % 2], picked[t][h][:], COPY, scale=rd_sb[:, t : t + 1])

        def words(pairs):
            return pairs[:].rearrange("p u m e -> p u (m e)").bitcast(F32).rearrange("p u m -> p m u")

        def quantise_page(c):
            codes = late.tile([P, BANK], I32, name="page_codes", bufs=4, align_bytes=64)
            nc.vector.quantize_mx(
                out=codes[:].bitcast(FP8X4), scales=page_scales[:, c * BANK : (c + 1) * BANK],
                in_=page_woven[c][:].rearrange("p m u -> p (m u)").bitcast(BF16),
            )
            nc.sync.dma_start(out_2[0].rearrange("p m i -> p (m i)").bitcast(I32)[:, c * BANK : (c + 1) * BANK], codes[:])

        def quantise_x(h):
            nc.vector.quantize_mx(
                out=x_codes[h][:].bitcast(FP8X4), scales=x_plane[h][:],
                in_=x_woven[h][:].rearrange("p m u -> p (m u)").bitcast(BF16),
            )

        def last_stage(h):
            cols = slice(h * BANK, (h + 1) * BANK)
            for b in range(N // P):
                rows = slice(b * P, (b + 1) * P)
                e = psum.tile([P, BANK], F32, name="e", tag="acc", bufs=6)
                nc.tensor.matmul_mx(e[:], lhsT=w4_codes[:, rows].bitcast(FP8X4), lhsT_scale=w4_plane[:, rows],
                                    rhs=x_codes[h][:].bitcast(FP8X4), rhs_scale=x_plane[h][:], start=True, stop=True)
                held = late.tile([P, BANK], F32, name="held", bufs=3)
                nc.vector.tensor_tensor(held[:], e[:], cush_sb[:, b, cols], MAX)
                scaled = late.tile([P, BANK], F32, name="scaled", bufs=3)
                nc.scalar.activation(scaled[:], held[:], COPY, scale=scl_sb[:, b : b + 1])
                nc.sync.dma_start(out_0[rows, cols], scaled[:])

        for b in range(BLOCKS):
            first_stage(b)
            if b % 2 == 1:
                turn(0, b - 1, b + 1)
                scatter(0, (b - 1) * P, (b + 1) * P)
        turn(1, 0, 4)
        turn(1, 4, 8)
        for t in range(PACK - 1):
            nc.sync.dma_start(page_rows_out[t], page[t][:])
            gather(t, 0)
            gather(t, 1)
            if t + 2 < PACK:
                turn(t + 2, 0, 4)
                turn(t + 2, 4, 8)
            for c in range(4):
                round_page(t, c)
            round_x(t, 0)
            round_x(t, 1)
            scatter(t + 1, 0, S)

        t = PACK - 1
        nc.sync.dma_start(page_rows_out[t], page[t][:])
        gather(t, 0)
        gather(t, 1)
        round_page(t, 0)
        round_page(t, 1)
        round_x(t, 0)
        round_x(t, 1)
        round_page(t, 2)
        round_page(t, 3)
        nc.vector.tensor_copy(page_woven[0][:], words(page_pairs[0]))
        nc.vector.tensor_copy(x_woven[0][:], words(x_pairs[0]))
        quantise_page(0)
        quantise_x(0)
        nc.vector.tensor_copy(x_woven[1][:], words(x_pairs[1]))
        nc.vector.tensor_copy(page_woven[1][:], words(page_pairs[1]))
        quantise_x(1)
        quantise_page(1)
        nc.scalar.copy(page_woven[2][:], words(page_pairs[2]))
        nc.scalar.copy(page_woven[3][:], words(page_pairs[3]))
        last_stage(0)
        quantise_page(2)
        quantise_page(3)
        for q in range(QUADS):
            nc.sync.dma_start(out_3[0, 4 * q : 4 * q + 4, :].bitcast(I32), page_scales[32 * q : 32 * q + 4, :].bitcast(I32))
        last_stage(1)
